import numpy as np, ml_dtypes
CORES = [36,164,52,180,100,228,116,244]
N = 8
BF = ml_dtypes.bfloat16
def gentries(a):
    return np.ascontiguousarray(a.reshape(8, 16, -1).transpose(0, 2, 1)).reshape(8, -1)
def gtable(e):
    e = np.asarray(e); return np.ascontiguousarray(e.reshape(8, -1, 16).transpose(0, 2, 1)).reshape(128, -1).astype(np.int32)
W, S, J, RO, LW = 4096, 32, 128, 8, 12
K = S * J
def pack(x, p, c):
    return {"ring": np.ascontiguousarray(x.reshape(N, 128, W)).astype(np.float32).astype(BF), "place": np.stack([gtable(a.reshape(8, K)) for a in p]),
            "carry": np.ascontiguousarray(c.reshape(N, 128, J)).astype(np.float32).astype(BF)}
def parts(rng):
    return rng.integers(0, 16, (N, 8, 16, W)), rng.integers(0, W, (N, 8, J, S)), rng.integers(0, 16, (N, 8, 16, J))
def extremes(rng, n):
    m = rng.integers(0, 4, (N, 8, 1, n))
    return np.where(m == 0, 0, np.where(m == 1, 15, 15 * rng.integers(0, 2, (N, 8, 16, n))))
def single(rng, hit):
    dig = rng.integers(0, 16, hit.shape)
    return (hit & (np.arange(16)[:, None] == dig)).astype(np.int64)
def setup_inputs(rng):
    x, p, c = parts(rng)
    return pack(x, p, c)
def setup_inputs_spread(rng):
    top = rng.choice(np.array([0, 1, 3, 7, 15]), (N, 8, 1, W)); x = ((top + 1) * rng.random((N, 8, 16, W))).astype(np.int64)
    top = rng.choice(np.array([0, 1, 3, 7, 15]), (N, 8, 1, J)); c = ((top + 1) * rng.random((N, 8, 16, J))).astype(np.int64)
    wd = 2 ** rng.integers(0, LW + 1, (N, 8, J, 1))
    p = (rng.integers(0, W, (N, 8, J, 1)) + (wd * rng.random((N, 8, J, S))).astype(np.int64)) & (W - 1)
    x[..., 5::16] = 15; x[..., 6::16] = 0; x[..., 7::16] = 8; h = 16 * rng.integers(0, W // 16, (N, 8, J, S))
    for j, a in ((0, 15), (2, 14), (J - 3, 14), (J - 1, 15)):
        c[:, :, :, j] = a; p[:, :, j] = h[:, :, j] + 5
    for j in (1, J - 2):
        c[:, :, :, j] = 0; p[:, :, j] = h[:, :, j] + 6; p[:, :, j, 0] += 1; p[:, :, j, S - 1] += 1
    return pack(x, p, c)
def setup_inputs_ends(rng):
    x = extremes(rng, W); c = extremes(rng, J); m = rng.integers(0, 4, (N, 8, J, 1))
    p = (W - 1) * np.where(m == 0, 0, np.where(m == 1, 1, rng.integers(0, 2, (N, 8, J, S))))
    x[:, 1::2, :, W - 1] = 15; x[:, 1::2, :, 0] = 0; x[:, 0::4, :, W - 1] = 0; x[:, 0::4, :, 0] = 15
    for j in (0, 3, J - 1):
        c[:, :, :, j] = 15; p[:, 1::2, j] = W - 1; p[:, 0::4, j] = 0
    for j in (1, 4, J - 2):
        c[:, :, :, j] = 0; p[:, 1::2, j] = 0; p[:, 0::4, j] = W - 1
    return pack(x, p, c)
def setup_inputs_corners(rng):
    x, p, c = parts(rng); run = np.arange(K).reshape(J, S) & (W - 1)
    for q in range(N):
        for g, m in enumerate(rng.permutation(8)):
            a = int(rng.integers(0, W))
            if m == 0: p[q, g] = a
            elif m == 1: p[q, g] = W - 1; c[q, g] = 15
            elif m == 2: p[q, g] = 0; c[q, g] = 0
            elif m == 3:
                p[q, g] = a; p[q, g, rng.integers(0, J), rng.integers(0, S)] = (a + 1 + rng.integers(0, W - 1)) & (W - 1)
            elif m == 4: p[q, g] = run
            elif m == 5: p[q, g] = W - 1 - run
            elif m == 6:
                x[q, g] = 0; x[q, g, :, W - 1] = 15; p[q, g] = rng.integers(-4, 4, (J, S)) & (W - 1)
            else:
                x[q, g] = 15; c[q, g, :, J - 1] = 15; c[q, g, :, J - 2] = 0
                s = np.add.reduce(c[q, g], axis=0); p[q, g, :, 0] = (W - s - (np.arange(J) & 1)) & (W - 1)
    return pack(x, p, c)
def setup_inputs_calm(rng):
    hit = rng.random((N, 8, 1, W)) < rng.choice(np.array([0.002, 0.008, 0.02]), (N, 8, 1, 1)); hit[..., :32] = False; hit[..., W - 8:] = False
    x = single(rng, hit); c = single(rng, rng.random((N, 8, 1, J)) < 0.25) * rng.integers(1, 4, (N, 8, 1, J))
    p = np.where(rng.random((N, 8, J, S)) < 0.5, rng.integers(-4, 4, (N, 8, J, S)) & (W - 1), rng.integers(0, W, (N, 8, J, S)))
    q = int(rng.integers(0, N)); g = int(rng.integers(0, 8)); c[q, g] = 0
    for t in range(RO):
        x[q, g] = 0; q = (q + 1 + t % (N - 1)) % N; g = (g + 1) % 8
    return pack(x, p, c)
def setup_inputs_full(rng):
    hit = rng.random((N, 8, 1, W)) < 0.004; top = 14 if S == 8 else 15
    for b in (0, 1): hit[..., (W - 1 - b + 240 * np.arange(-RO, RO + 1)) & (W - 1)] = False
    hit[:, 1::2, :, 15::16] = False
    x = single(rng, hit); x[:, 0::2] = 15 * x[:, 0::2]; x[:, 1::2] = top - x[:, 1::2]
    c = 15 - single(rng, rng.random((N, 8, 1, J)) < 0.125)
    late = (W - 1 - rng.integers(0, 2, (N, 8, J, S)) - 240 * rng.integers(0, RO, (N, 8, J, S))) & (W - 1)
    p = np.where(rng.random((N, 8, J, S)) < 0.5, late, rng.integers(0, W, (N, 8, J, S)))
    e = (W - 1 + 240 * (RO - 1)) & (W - 1); x[:, 0::2, :, e] = 7; x[:, 1::2, :, e] = 3
    c[:, :, :, J - 1] = 15; p[:, 1::2, J - 1] = W - 1; p[:, 0::2, J - 1] = late[:, 0::2, J - 1]; p[:, 0::2, J - 1, 0] = W - 1; p[:, 0::2, J - 1, S - 1] = W - 1
    return pack(x, p, c)
def check_inputs(d):
    bad = []
    for k, lo, hi in (("ring", 0, 15), ("place", 0, W - 1), ("carry", 0, 15)):
        a = np.asarray(d[k]).astype(np.float64)
        if not (np.min(a) >= lo and np.max(a) <= hi): bad.append("range of " + k)
        if np.any(a != np.floor(a)): bad.append("whole numbers in " + k)
    return bad
def reference(ring, place, carry):
    x = ring.astype(np.float32).astype(np.int32).reshape(N, 8, 16, W); c = carry.astype(np.float32).astype(np.int32).reshape(N, 8, 16, J)
    p = np.stack([gentries(a) for a in place]).astype(np.int64); shown = []
    for t in range(RO):
        v = np.take_along_axis(x, p[:, :, None, :], 3).reshape(N, 8, 16, J, S)
        after = (c[..., None] + np.add.accumulate(v, axis=4, dtype=np.int32)) & 15
        into = np.concatenate([c[..., None], after[..., :S - 1]], axis=4)
        p = (p + np.add.reduce(into, axis=2).reshape(N, 8, K)) & (W - 1)
        end = np.ascontiguousarray(after[..., S - 1]); shown.append(end.reshape(N, 128, J))
        c = np.roll(end, (1 + t % (N - 1), 1), axis=(0, 1))
    return {"yp": np.stack([gtable(a) for a in p]).astype(np.float32), "yc": np.concatenate(shown, axis=2).astype(np.float32).astype(BF)}

@@ -1,0 +1,308 @@
+from concourse.mybir import AluOpType, ActivationFunctionType
+
+NR, W, S, J, RO = 8, 4096, 32, 128, 8
+CH = (44,42,42)
+ND = (3,2,2)
+ND0 = 22
+NDL = 3
+GI = 0
+ORD = 0
+NC = len(CH)
+J0 = [sum(CH[:c]) for c in range(NC + 1)]
+JM = max(CH)
+EXT = 240 * (RO - 1)
+QOFF = 2064.0
+CM = 16 * QOFF
+BIG = 4096.0
+
+SCRATCH = {
+    "win": ("sbuf", [128, W + EXT], "bfloat16"),
+    "pli": ("sbuf", [128, 256], "int32"),
+    "plf": ("sbuf", [128, 256], "float32"),
+    "off": ("sbuf", [128, 256], "uint16"),
+    "xs": ("sbuf", [128, S * J], "bfloat16"),
+    "vs": ("sbuf", [128, S * J], "float16"),
+    "qs": ("sbuf", [128, S * J], "bfloat16"),
+    "msk": ("sbuf", [128, S * J], "bfloat16"),
+    "land": ("sbuf", [128, RO * J], "bfloat16"),
+    "ycs": ("sbuf", [128, RO * J], "bfloat16"),
+    "tmp": ("sbuf", [128, 2 * JM], "float32"),
+    "yo": ("sbuf", [128, 256], "float32"),
+    "pcol": ("sbuf", [128, 1], "int32"),
+    "gint": ("sbuf", [128, 1], "int32"),
+    "g15": ("sbuf", [128, 1], "float32"),
+    "idf": ("sbuf", [128, 128], "bfloat16"),
+    "iw": ("sbuf", [128, 144], "bfloat16"),
+    "wv": ("sbuf", [128, 144], "float16"),
+    "wq": ("sbuf", [128, 144], "bfloat16"),
+    "wl": ("sbuf", [128, 144], "bfloat16"),
+    "kq": ("sbuf", [128, JM], "bfloat16"),
+    "sa": ("sbuf", [128, 128], "float16"),
+    "sb": ("sbuf", [128, 128], "float16"),
+    "sh": ("sbuf", [128, 128], "float16"),
+    "nsh": ("sbuf", [128, 128], "bfloat16"),
+    "idn": ("sbuf", [128, 128], "float32"),
+    "pc0": ("psum", [128, 512], "float32"),
+    "pc1": ("psum", [128, 512], "float32"),
+}
+for _c in range(NC):
+    SCRATCH["pp%d" % _c] = ("psum", [128, 512], "float32")
+SEMAPHORES = (["sV", "sP", "sA", "sG", "dring", "dext", "dplace", "dcarry", "stored", "sent"]
+              + ["arr%d_%d" % (t, c) for t in range(1, RO) for c in range(NC)])
+
+
+def rank_program(g, core, T, topo):
+    rank = T.rank_of(core)
+    if rank is None:
+        return
+    A = AluOpType
+    queue = {"V": g.vector, "P": g.tensor, "A": g.scalar, "G": g, "S": g.sync}
+    known = {e: {} for e in queue}
+    count = {}
+    lastw, readers = {}, {}
+    serial = [0]
+
+    def wait(e, tok):
+        _, name, val, clock, _e = tok
+        if known[e].get(name, 0) >= val:
+            return
+        queue[e].wait_ge(T.sem[name], val)
+        known[e][name] = val
+        for k, v in clock.items():
+            if known[e].get(k, 0) < v:
+                known[e][k] = v
+
+    def op(e, fn, reads, writes, sem=None, n=1):
+        toks = [lastw[k] for k in list(reads) + list(writes) if k in lastw]
+        toks += [t for k in writes for t in readers.get(k, [])]
+        for tok in sorted(toks, key=lambda t: -t[0]):
+            if e == "P" and tok[4] == "P":
+                continue
+            wait(e, tok)
+        ins = fn()
+        if ins is None:
+            return
+        name = sem or "s" + e
+        ins.then_inc(T.sem[name], n)
+        count[name] = count.get(name, 0) + n
+        serial[0] += 1
+        tok = (serial[0], name, count[name], dict(known[e]), e)
+        for k in reads:
+            readers.setdefault(k, []).append(tok)
+        for k in writes:
+            lastw[k] = tok
+            readers[k] = []
+
+    V, P = g.vector, g.tensor
+    pp = [T["pp%d" % c] for c in range(NC)]
+    NQ = RO * NC
+
+    def span(i, m):
+        c = i % NC
+        return m * J0[c], m * J0[c + 1]
+
+    def cols(i):
+        t, c = divmod(i, NC)
+        return t * J + J0[c], t * J + J0[c + 1]
+
+    op("S", lambda: g.sync.dma_start(T.win[:, 0:W], T.ring[:]), [], ["win"], "dring", 16)
+    op("A", lambda: g.scalar.dma_start(T.pli[:], T.place[:]), [], ["pli"], "dplace", 16)
+    op("A", lambda: g.scalar.dma_start(T.land[:, 0:J], T.carry[:]), [], [("land", c) for c in range(NC)], "dcarry", 16)
+    op("S", lambda: g.sync.dma_start(T.win[:, W:W + EXT], T.ring[:, 0:EXT]), [], ["ext"], "dext", 16)
+    for i in range(NC, NQ):
+        t, c = divmod(i, NC)
+        src = T.cores[(rank - 1 - (t - 1) % (NR - 1)) % NR]
+        serial[0] += 1
+        lastw[("land", i)] = (serial[0], "arr%d_%d" % (t, c), len(topo.engines(src, core)), {}, "R")
+
+    def iota(name, pattern, cm):
+        op("G", lambda: g.iota(T[name][:], pattern, 0, cm, allow_small_or_imprecise_dtypes=True), [], [name])
+
+    def scal(out, in0, s1, o1, s2=None, o2=None):
+        col = [s1] if isinstance(s1, str) else []
+        a1 = T[s1][:] if col else s1
+        if o2 is None:
+            op("V", lambda: V.tensor_scalar(T[out][:], T[in0][:], a1, None, o1), [in0] + col, [out])
+        else:
+            op("V", lambda: V.tensor_scalar(T[out][:], T[in0][:], a1, s2, o1, o2), [in0] + col, [out])
+
+    op("G", lambda: g.iota(T.pcol[:], [[0, 1]], 0, 1), [], ["pcol"])
+    iota("iw", [[1, 144]], 0)
+    iota("idf", [[1, 128]], -1)
+    a, b = span(0, S)
+    op("V", lambda: V.memset(T.msk[:, a:b], BIG), [], [("msk", 0)])
+    scal("gint", "pcol", 112, A.bitwise_and)
+    op("V", lambda: V.memset(T.kq[:], QOFF), [], ["kq"])
+    scal("g15", "gint", 15.0, A.add)
+    scal("idn", "idf", 0.0, A.is_equal)
+    scal("sa", "idf", 16.0, A.is_equal)
+    scal("sb", "idf", -112.0, A.is_equal)
+    scal("wv", "iw", "g15", A.is_equal)
+    scal("wl", "iw", "g15", A.is_equal)
+    scal("wq", "iw", "g15", A.is_equal, -1.0, A.mult)
+    op("V", lambda: V.tensor_tensor(T.sh[:], T.sa[:], T.sb[:], A.add), ["sa", "sb"], ["sh"])
+    op("V", lambda: V.memset(T.msk[:, b:S * J], BIG), [], [("msk", c) for c in range(1, NC)])
+    scal("nsh", "sh", -1.0, A.mult)
+    op("V", lambda: V.tensor_copy(T.off[:], T.pli[:]), ["pli"], [("off", c) for c in range(NC)])
+    op("V", lambda: V.tensor_scalar(T.plf[:], T.pli[:], RO * CM, None, A.add), ["pli"], [("plf", c) for c in range(NC)])
+
+    def nd(i):
+        return ND0 if i == 0 else NDL if i == NQ - 1 else ND[i % NC]
+
+    def gather(e, i):
+        t, c = divmod(i, NC)
+        a, b = (J0[c], J0[c + 1] - nd(i)) if e == "A" else (J0[c + 1] - nd(i), J0[c + 1])
+        if a == b:
+            return
+        out = T.xs[:, S * a:S * b]
+        src = T.win[:, 0:W + 240 * t].indirect(T.off[:, 2 * a:2 * b])
+        reads = ["win", ("off", c)] + (["ext"] if t else [])
+        if e == "A":
+            op("A", lambda: g.scalar.activation(out, src, ActivationFunctionType.Identity, bias=16.0), reads,
+               [("xa", c)] + ([] if nd(i) else [("xv", c)]))
+        else:
+            op("V", lambda: V.tensor_scalar(out, src, 16.0, None, A.add), reads, [("xv", c)])
+
+    def inject(i):
+        a, b = span(i, S)
+        l, r = cols(i)
+        if GI and i >= NC:
+            op("G", lambda: g.affine_select(T.msk[:, a:b:S], T.land[:, l:r], [[0, r - l]], A.is_ge, 0.0, 0, 0),
+               [("land", i)], [("msk", i % NC)])
+        else:
+            op("V", lambda: V.tensor_copy(T.msk[:, a:b:S], T.land[:, l:r]), [("land", i)], [("msk", i % NC)])
+
+    def scan(i):
+        c = i % NC
+        a, b = span(i, S)
+        op("V", lambda: V.tensor_tensor_scan(T.vs[:, a:b], T.msk[:, a:b], T.xs[:, a:b], BIG, A.min, A.add),
+           [("msk", c), ("xa", c), ("xv", c)], [("v", c)])
+
+    def floor16(i):
+        c = i % NC
+        a, b = span(i, S)
+        op("V", lambda: V.tensor_scalar(T.qs[:, a:b], T.vs[:, a:b], QOFF - 7.5, None, A.add), [("v", c)], [("q", c)])
+
+    def sums(i, w, buf, first, last):
+        c = i % NC
+        a, b = span(i, S)
+        n = 2 * CH[c]
+        for r in range(1, 16):
+            P.matmul(pp[c][:, 0:n], w[:, 15 - r:143 - r], buf[:, a + r - 1:b:16], first and r == 1, False)
+        return P.matmul(pp[c][:, 1:n:2], w[:, 15:143], buf[:, a + 15:b:S], False, last)
+
+    def mm_old(i):
+        c = i % NC
+        a, b = span(i, 2)
+        op("P", lambda: P.matmul(pp[c][:, 0:b - a], T.idn[:], T.plf[:, a:b], True, False), ["idn", ("plf", c)], [("pp", c)])
+
+    def mm_v(i):
+        c = i % NC
+        l, r = cols(i)
+
+        def f():
+            sums(i, T.wv, T.vs, i < NQ - NC, False)
+            P.matmul(pp[c][:, 0:2 * CH[c]:2], T.wl[:, 15:143], T.land[:, l:r], False, False)
+            return P.matmul(pp[c][:, 0:2 * CH[c]:2], T.wq[:, 15:143], T.kq[:, 0:CH[c]], False, False)
+        op("P", f, ["wl", "wq", "wv", "kq", ("land", i), ("v", c)], [("pp", c)])
+
+    def mm_q(i):
+        op("P", lambda: sums(i, T.wq, T.qs, False, True), ["wq", ("q", i % NC)], [("pp", i % NC)])
+
+    def mm_c(i):
+        c = i % NC
+        a, b = span(i, S)
+        pc = "pc%d" % (i % 2)
+
+        def f():
+            P.matmul(T[pc][:, 0:CH[c]], T.sh[:], T.vs[:, a + S - 1:b:S], True, False)
+            return P.matmul(T[pc][:, 0:CH[c]], T.nsh[:], T.qs[:, a + S - 1:b:S], False, True)
+        op("P", f, ["sh", "nsh", ("v", c), ("q", c)], [pc])
+
+    def ev_c(i):
+        l, r = cols(i)
+        pc = "pc%d" % (i % 2)
+        op("V", lambda: V.tensor_scalar(T.ycs[:, l:r], T[pc][:, 0:r - l], QOFF, None, A.add), [], [pc, ("ycs", i)])
+
+    nsent = [0]
+
+    def send(i):
+        t, c = divmod(i, NC)
+        dst = T.cores[(rank + 1 + t % (NR - 1)) % NR]
+        rid, pid = topo.addr(dst, core)
+        l, r = cols(i)
+
+        def f():
+            g.remote_dma(T.land[:, l + J:r + J], T.ycs[:, l:r], T.sem["arr%d_%d" % (t + 1, c)], T.sem.sent,
+                         pid, rid, topo.mask(core, dst))
+            nsent[0] += len(topo.engines(core, dst))
+        op("G", f, [("ycs", i)], [])
+
+    def ev_p(i):
+        t, c = divmod(i, NC)
+        a, b = span(i, 2)
+        if t < RO - 1:
+            op("V", lambda: V.tensor_tensor(T.plf[:, a:b], pp[c][:, 0:b - a], T.plf[:, a:b], A.add),
+               [], [("pp", c), ("plf", c)])
+        else:
+            op("V", lambda: V.tensor_scalar(T.tmp[:, 0:b - a], pp[c][:, 0:b - a], float(W), float(W), A.is_ge, A.mult),
+               [], [("pp", c), "tmp"])
+
+    def ev_o(i):
+        t, c = divmod(i, NC)
+        a, b = span(i, 2)
+        if t < RO - 1:
+            op("V", lambda: V.tensor_scalar(T.off[:, a:b], T.plf[:, a:b], -(RO - 1 - t) * CM, None, A.add),
+               [("plf", c)], [("off", c)])
+            return
+        op("V", lambda: V.tensor_tensor(T.yo[:, a:b], pp[c][:, 0:b - a], T.tmp[:, 0:b - a], A.subtract),
+           ["tmp"], [("pp", c), ("yo", c)])
+        if c >= NC - 2:
+            c0 = 0 if c == NC - 2 else c
+            op("S", lambda: g.sync.dma_start(T.yp[:, 2 * J0[c0]:b], T.yo[:, 2 * J0[c0]:b]),
+               [("yo", k) for k in range(c0, c + 1)], [], "stored", 16)
+
+    def store_c(e, i0, i1):
+        cs = slice(cols(i0)[0], cols(i1 - 1)[1])
+        keys = [("ycs", k) for k in range(i0, i1)]
+        op(e, lambda: queue[e].dma_start(T.yc[0:112, cs], T.ycs[16:128, cs]), keys, [], "stored", 16)
+        op(e, lambda: queue[e].dma_start(T.yc[112:128, cs], T.ycs[0:16, cs]), keys, [], "stored", 16)
+
+    gather("A", 0)
+    gather("V", 0)
+    inject(0)
+    def out_c(i):
+        ev_c(i)
+        if i < NQ - NC:
+            send(i)
+        if i == NQ - 3:
+            store_c("S", 0, NQ - 2)
+        if i == NQ - 1:
+            store_c("A", NQ - 2, NQ)
+
+    for i in range(NQ):
+        more = i + 1 < NQ
+        if i >= NQ - NC:
+            mm_old(i)
+        scan(i)
+        mm_v(i)
+        if i >= 1:
+            ev_p(i - 1)
+            if ORD == 1:
+                ev_o(i - 1)
+        floor16(i)
+        mm_c(i)
+        mm_q(i)
+        if i >= 1 and ORD == 0:
+            ev_o(i - 1)
+        if more:
+            gather("V", i + 1)
+            gather("A", i + 1)
+            inject(i + 1)
+        out_c(i)
+    ev_p(NQ - 1)
+    ev_o(NQ - 1)
+
+    g.wait_ge(T.sem.sent, nsent[0])
+    for name in ("sG", "sA", "sP", "sV", "stored"):
+        g.wait_ge(T.sem[name], count[name])

@@ -1,19 +1,20 @@
 from concourse.mybir import AluOpType, ActivationFunctionType
 
 NR, W, S, J, RO = 8, 4096, 32, 128, 8
-CH = (44,42,42)
-ND = (3,2,2)
-ND0 = 22
-NDL = 3
-GI = 0
-ORD = 0
+CH = (44, 42, 42)
+ND = (9, 9, 9)
+ND0 = (21, 7, 7)
+NDL = (9, 7, 5)
 NC = len(CH)
 J0 = [sum(CH[:c]) for c in range(NC + 1)]
 JM = max(CH)
 EXT = 240 * (RO - 1)
-QOFF = 2064.0
-CM = 16 * QOFF
-BIG = 4096.0
+U = 2.0 ** -28
+UP = 2.0 ** 24
+HALF = 7.5
+LIFT = 64.0
+NY = RO * J - CH[-1]
+SHOW = {4 * NC: (0, 4 * J), (RO - 1) * NC: (4 * J, (RO - 1) * J), RO * NC - 1: ((RO - 1) * J, NY)}
 
 SCRATCH = {
     "win": ("sbuf", [128, W + EXT], "bfloat16"),
@@ -21,32 +22,35 @@ SCRATCH = {
     "plf": ("sbuf", [128, 256], "float32"),
     "off": ("sbuf", [128, 256], "uint16"),
     "xs": ("sbuf", [128, S * J], "bfloat16"),
-    "vs": ("sbuf", [128, S * J], "float16"),
-    "qs": ("sbuf", [128, S * J], "bfloat16"),
-    "msk": ("sbuf", [128, S * J], "bfloat16"),
+    "vs": ("sbuf", [128, S * J + 16 * NC], "float16"),
+    "msk": ("sbuf", [128, S * JM], "bfloat16"),
+    "cin": ("sbuf", [128, J], "bfloat16"),
     "land": ("sbuf", [128, RO * J], "bfloat16"),
+    "snd": ("sbuf", [128, NY], "bfloat16"),
+    "us": ("sbuf", [128, NY], "float16"),
+    "ycu": ("sbuf", [128, NY], "bfloat16"),
     "ycs": ("sbuf", [128, RO * J], "bfloat16"),
-    "tmp": ("sbuf", [128, 2 * JM], "float32"),
+    "ds": ("sbuf", [128, 2 * JM], "float16"),
+    "tmp": ("sbuf", [128, 256], "float32"),
+    "tmc": ("sbuf", [128, CH[-1]], "float32"),
     "yo": ("sbuf", [128, 256], "float32"),
     "pcol": ("sbuf", [128, 1], "int32"),
     "gint": ("sbuf", [128, 1], "int32"),
+    "rint": ("sbuf", [128, 1], "int32"),
     "g15": ("sbuf", [128, 1], "float32"),
+    "gnum": ("sbuf", [128, 1], "float32"),
+    "not0": ("sbuf", [128, 1], "float32"),
+    "back": ("sbuf", [128, 1], "float32"),
     "idf": ("sbuf", [128, 128], "bfloat16"),
     "iw": ("sbuf", [128, 144], "bfloat16"),
-    "wv": ("sbuf", [128, 144], "float16"),
     "wq": ("sbuf", [128, 144], "bfloat16"),
     "wl": ("sbuf", [128, 144], "bfloat16"),
-    "kq": ("sbuf", [128, JM], "bfloat16"),
-    "sa": ("sbuf", [128, 128], "float16"),
-    "sb": ("sbuf", [128, 128], "float16"),
-    "sh": ("sbuf", [128, 128], "float16"),
-    "nsh": ("sbuf", [128, 128], "bfloat16"),
     "idn": ("sbuf", [128, 128], "float32"),
-    "pc0": ("psum", [128, 512], "float32"),
-    "pc1": ("psum", [128, 512], "float32"),
 }
-for _c in range(NC):
-    SCRATCH["pp%d" % _c] = ("psum", [128, 512], "float32")
+for _n in ("ig", "sa", "shx", "shq", "shv", "one", "ones", "onex", "tri"):
+    SCRATCH[_n] = ("sbuf", [128, 128], "bfloat16")
+for _n in ["pc0", "pc1", "pd0", "pd1"] + ["pp%d" % _c for _c in range(NC)]:
+    SCRATCH[_n] = ("psum", [128, 512], "float32")
 SEMAPHORES = (["sV", "sP", "sA", "sG", "dring", "dext", "dplace", "dcarry", "stored", "sent"]
               + ["arr%d_%d" % (t, c) for t in range(1, RO) for c in range(NC)])
 
@@ -56,6 +60,7 @@ def rank_program(g, core, T, topo):
     if rank is None:
         return
     A = AluOpType
+    Ident = ActivationFunctionType.Identity
     queue = {"V": g.vector, "P": g.tensor, "A": g.scalar, "G": g, "S": g.sync}
     known = {e: {} for e in queue}
     count = {}
@@ -96,18 +101,23 @@ def rank_program(g, core, T, topo):
     V, P = g.vector, g.tensor
     pp = [T["pp%d" % c] for c in range(NC)]
     NQ = RO * NC
+    every = range(NC)
 
     def span(i, m):
         c = i % NC
         return m * J0[c], m * J0[c + 1]
 
+    def vspan(i):
+        a, b = span(i, S)
+        return a + 16 * (i % NC + 1), b + 16 * (i % NC + 1)
+
     def cols(i):
         t, c = divmod(i, NC)
         return t * J + J0[c], t * J + J0[c + 1]
 
-    op("S", lambda: g.sync.dma_start(T.win[:, 0:W], T.ring[:]), [], ["win"], "dring", 16)
     op("A", lambda: g.scalar.dma_start(T.pli[:], T.place[:]), [], ["pli"], "dplace", 16)
-    op("A", lambda: g.scalar.dma_start(T.land[:, 0:J], T.carry[:]), [], [("land", c) for c in range(NC)], "dcarry", 16)
+    op("S", lambda: g.sync.dma_start(T.win[:, 0:W], T.ring[:]), [], ["win"], "dring", 16)
+    op("A", lambda: g.scalar.dma_start(T.cin[:], T.carry[:]), [], ["cin"], "dcarry", 16)
     op("S", lambda: g.sync.dma_start(T.win[:, W:W + EXT], T.ring[:, 0:EXT]), [], ["ext"], "dext", 16)
     for i in range(NC, NQ):
         t, c = divmod(i, NC)
@@ -126,103 +136,147 @@ def rank_program(g, core, T, topo):
         else:
             op("V", lambda: V.tensor_scalar(T[out][:], T[in0][:], a1, s2, o1, o2), [in0] + col, [out])
 
+    def times(out, in0, k):
+        op("A", lambda: g.scalar.activation(T[out][:], T[in0][:], Ident, scale=k), [in0], [out])
+
+    def keep(out, in0, cmp, fill, base):
+        op("G", lambda: g.affine_select(T[out][:], T[in0][:], [[1, 128]], cmp, fill, base, -1), [in0], [out])
+
+    def gcopy(out, in_, n, reads, writes):
+        op("G", lambda: g.affine_select(out, in_, [[0, n]], A.is_ge, 0.0, 0, 0), reads, writes)
+
     op("G", lambda: g.iota(T.pcol[:], [[0, 1]], 0, 1), [], ["pcol"])
     iota("iw", [[1, 144]], 0)
+    iota("ig", [[16, 8], [0, 16]], 0)
     iota("idf", [[1, 128]], -1)
-    a, b = span(0, S)
-    op("V", lambda: V.memset(T.msk[:, a:b], BIG), [], [("msk", 0)])
+    op("V", lambda: V.memset(T.msk[:], 1.0), [], ["msk"])
     scal("gint", "pcol", 112, A.bitwise_and)
-    op("V", lambda: V.memset(T.kq[:], QOFF), [], ["kq"])
+    scal("rint", "pcol", 15, A.bitwise_and)
+    op("V", lambda: V.memset(T.msk[:, 0:S * JM:S], 0.0), [], ["msk"])
     scal("g15", "gint", 15.0, A.add)
-    scal("idn", "idf", 0.0, A.is_equal)
+    scal("gnum", "gint", 0.0, A.add)
+    scal("not0", "rint", 0.0, A.is_gt)
+    scal("wl", "iw", "g15", A.is_equal, 1 / U, A.mult)
+    scal("one", "ig", "gnum", A.is_equal)
+    scal("back", "rint", 0.0, A.is_equal, 16 * HALF, A.mult)
     scal("sa", "idf", 16.0, A.is_equal)
-    scal("sb", "idf", -112.0, A.is_equal)
-    scal("wv", "iw", "g15", A.is_equal)
-    scal("wl", "iw", "g15", A.is_equal)
-    scal("wq", "iw", "g15", A.is_equal, -1.0, A.mult)
-    op("V", lambda: V.tensor_tensor(T.sh[:], T.sa[:], T.sb[:], A.add), ["sa", "sb"], ["sh"])
-    op("V", lambda: V.memset(T.msk[:, b:S * J], BIG), [], [("msk", c) for c in range(1, NC)])
-    scal("nsh", "sh", -1.0, A.mult)
-    op("V", lambda: V.tensor_copy(T.off[:], T.pli[:]), ["pli"], [("off", c) for c in range(NC)])
-    op("V", lambda: V.tensor_scalar(T.plf[:], T.pli[:], RO * CM, None, A.add), ["pli"], [("plf", c) for c in range(NC)])
+    scal("ones", "one", "not0", A.mult)
+    op("V", lambda: V.memset(T.msk[:, S - 1:S * JM:S], UP), [], ["msk"])
+    op("V", lambda: V.tensor_copy(T.off[:], T.pli[:]), ["pli"], [("off", c) for c in every])
+    keep("shx", "sa", A.not_equal, 1.0, 112)
+    keep("tri", "one", A.is_ge, 0.0, 0)
+    times("wq", "wl", -1.0)
+    times("onex", "one", 1 / U)
+    times("shq", "shx", -1.0)
+    times("shv", "shx", 1 / UP)
+    gcopy(T.plf[:], T.pli[:], 2 * J, ["pli"], [("plf", c) for c in every])
+    keep("idn", "one", A.is_equal, 0.0, 0)
 
     def nd(i):
-        return ND0 if i == 0 else NDL if i == NQ - 1 else ND[i % NC]
+        return ND0[i] if i < NC else NDL[i % NC] if i >= NQ - NC else ND[i % NC]
 
     def gather(e, i):
         t, c = divmod(i, NC)
         a, b = (J0[c], J0[c + 1] - nd(i)) if e == "A" else (J0[c + 1] - nd(i), J0[c + 1])
-        if a == b:
-            return
         out = T.xs[:, S * a:S * b]
         src = T.win[:, 0:W + 240 * t].indirect(T.off[:, 2 * a:2 * b])
         reads = ["win", ("off", c)] + (["ext"] if t else [])
         if e == "A":
-            op("A", lambda: g.scalar.activation(out, src, ActivationFunctionType.Identity, bias=16.0), reads,
-               [("xa", c)] + ([] if nd(i) else [("xv", c)]))
+            op("A", lambda: g.scalar.activation(out, src, Ident, scale=U), reads, [("xa", c)])
         else:
-            op("V", lambda: V.tensor_scalar(out, src, 16.0, None, A.add), reads, [("xv", c)])
+            op("V", lambda: V.tensor_scalar(out, src, U, None, A.mult), reads, [("xv", c)])
 
-    def inject(i):
+    def cast(i):
+        l, r = cols(i)
+        a, b = vspan(i)
+        gcopy(T.vs[:, a - 1:b - 1:S], T.land[:, l:r], r - l, [("land", i)], [("vt", i % NC)])
+
+    def xk(i):
+        return [("xa", i % NC), ("xv", i % NC)]
+
+    def fix(i):
         a, b = span(i, S)
         l, r = cols(i)
-        if GI and i >= NC:
-            op("G", lambda: g.affine_select(T.msk[:, a:b:S], T.land[:, l:r], [[0, r - l]], A.is_ge, 0.0, 0, 0),
-               [("land", i)], [("msk", i % NC)])
-        else:
-            op("V", lambda: V.tensor_copy(T.msk[:, a:b:S], T.land[:, l:r]), [("land", i)], [("msk", i % NC)])
+        op("V", lambda: V.tensor_tensor_scan(T.xs[:, a:b:S], T.xs[:, a:b:S], T.land[:, l:r], 1.0, A.min, A.add),
+           [("land", i)] + xk(i), [("x0", i % NC)])
 
     def scan(i):
-        c = i % NC
         a, b = span(i, S)
-        op("V", lambda: V.tensor_tensor_scan(T.vs[:, a:b], T.msk[:, a:b], T.xs[:, a:b], BIG, A.min, A.add),
-           [("msk", c), ("xa", c), ("xv", c)], [("v", c)])
-
-    def floor16(i):
-        c = i % NC
-        a, b = span(i, S)
-        op("V", lambda: V.tensor_scalar(T.qs[:, a:b], T.vs[:, a:b], QOFF - 7.5, None, A.add), [("v", c)], [("q", c)])
-
-    def sums(i, w, buf, first, last):
-        c = i % NC
-        a, b = span(i, S)
-        n = 2 * CH[c]
-        for r in range(1, 16):
-            P.matmul(pp[c][:, 0:n], w[:, 15 - r:143 - r], buf[:, a + r - 1:b:16], first and r == 1, False)
-        return P.matmul(pp[c][:, 1:n:2], w[:, 15:143], buf[:, a + 15:b:S], False, last)
+        l, r = vspan(i)
+        op("V", lambda: V.tensor_tensor_scan(T.vs[:, l:r], T.msk[:, 0:b - a], T.xs[:, a:b], 0.0, A.mult, A.add),
+           ["msk", ("x0", i % NC)] + xk(i), [("v", i % NC), ("vt", i % NC)])
 
     def mm_old(i):
         c = i % NC
         a, b = span(i, 2)
         op("P", lambda: P.matmul(pp[c][:, 0:b - a], T.idn[:], T.plf[:, a:b], True, False), ["idn", ("plf", c)], [("pp", c)])
 
-    def mm_v(i):
+    def mm_x(i, stages):
         c = i % NC
-        l, r = cols(i)
+        a, b = span(i, S)
+        pd = "pd%d" % (i % 2)
 
         def f():
-            sums(i, T.wv, T.vs, i < NQ - NC, False)
-            P.matmul(pp[c][:, 0:2 * CH[c]:2], T.wl[:, 15:143], T.land[:, l:r], False, False)
-            return P.matmul(pp[c][:, 0:2 * CH[c]:2], T.wq[:, 15:143], T.kq[:, 0:CH[c]], False, False)
-        op("P", f, ["wl", "wq", "wv", "kq", ("land", i), ("v", c)], [("pp", c)])
+            for r in stages:
+                ins = P.matmul(T[pd][:, 0:2 * CH[c]], T.wl[:, 14 - r:142 - r], T.xs[:, a + r:b:16], r == 1, r == 0)
+            return ins
+        op("P", f, ["wl"] + xk(i) + ([("x0", c)] if 0 in stages else []), [pd])
+
+    def ev_d(i):
+        pd, n = "pd%d" % (i % 2), 2 * CH[i % NC]
+        op("V", lambda: V.tensor_scalar(T.ds[:, 0:n], T[pd][:, 0:n], T.back[:], None, A.add), ["back"], [pd, "ds"])
+
+    def mm_s(i):
+        c = i % NC
+        a, b = vspan(i)
+        l, r = cols(i)
+        n = 2 * CH[c]
+
+        def f():
+            P.matmul(pp[c][:, 0:n:2], T.wl[:, 15:143], T.land[:, l:r], False, False)
+            P.matmul(pp[c][:, 1:n:2], T.onex[:], T.xs[:, S * J0[c] + 15:S * J0[c + 1]:S], False, False)
+            P.matmul(pp[c][:, 0:n], T.wq[:, 15:143], T.vs[:, a - 1:b - 1:16], False, False)
+            P.matmul(pp[c][:, 1:n:2], T.ones[:], T.ds[:, 0:n:2], False, False)
+            return P.matmul(pp[c][:, 0:n], T.tri[:], T.ds[:, 0:n], False, True)
+        op("P", f, ["wq", "wl", "onex", "ones", "tri", "ds", ("land", i), ("v", c), ("vt", c)] + xk(i), [("pp", c)])
 
     def mm_q(i):
-        op("P", lambda: sums(i, T.wq, T.qs, False, True), ["wq", ("q", i % NC)], [("pp", i % NC)])
+        c = i % NC
+        a, b = vspan(i)
+        n = 2 * CH[c]
+
+        def f():
+            for r in range(1, 16):
+                ins = P.matmul(pp[c][:, 0:n], T.wq[:, 15 - r:143 - r], T.vs[:, a + r - 1:b:16], r == 1 and i < NQ - 1, False)
+            return ins
+        op("P", f, ["wq", ("v", c)], [("pp", c)])
 
     def mm_c(i):
         c = i % NC
         a, b = span(i, S)
+        l, r = vspan(i)
         pc = "pc%d" % (i % 2)
 
         def f():
-            P.matmul(T[pc][:, 0:CH[c]], T.sh[:], T.vs[:, a + S - 1:b:S], True, False)
-            return P.matmul(T[pc][:, 0:CH[c]], T.nsh[:], T.qs[:, a + S - 1:b:S], False, True)
-        op("P", f, ["sh", "nsh", ("v", c), ("q", c)], [pc])
+            P.matmul(T[pc][:, 0:CH[c]], T.shx[:], T.xs[:, a + S - 1:b:S], True, False)
+            P.matmul(T[pc][:, 0:CH[c]], T.shv[:], T.vs[:, l + S - 1:r:S], False, False)
+            return P.matmul(T[pc][:, 0:CH[c]], T.shq[:], T.vs[:, l + S - 2:r:S], False, True)
+        op("P", f, ["shx", "shv", "shq"] + xk(i) + [("v", c), ("vt", c)], [pc])
 
     def ev_c(i):
         l, r = cols(i)
         pc = "pc%d" % (i % 2)
-        op("V", lambda: V.tensor_scalar(T.ycs[:, l:r], T[pc][:, 0:r - l], QOFF, None, A.add), [], [pc, ("ycs", i)])
+        op("V", lambda: V.tensor_scalar(T.snd[:, l:r], T[pc][:, 0:r - l], LIFT * U, None, A.add), [], [pc, ("snd", i)])
+
+    def last_c(k):
+        n, pc = CH[-1], "pc%d" % ((NQ - 1) % 2)
+        if k == 0:
+            op("V", lambda: V.tensor_scalar(T.tmc[:], T[pc][:, 0:n], 8 * U, 16 * U, A.is_ge, A.mult), [], [pc, "tmc"])
+        if k == 1:
+            op("V", lambda: V.tensor_tensor(T.tmc[:], T[pc][:, 0:n], T.tmc[:], A.subtract), [], [pc, "tmc"])
+        if k == 2:
+            op("V", lambda: V.tensor_scalar(T.ycs[:, NY:RO * J], T.tmc[:], 1 / U, HALF, A.mult, A.add), ["tmc"],
+               [("ycs", NQ - 1)])
 
     nsent = [0]
 
@@ -233,75 +287,112 @@ def rank_program(g, core, T, topo):
         l, r = cols(i)
 
         def f():
-            g.remote_dma(T.land[:, l + J:r + J], T.ycs[:, l:r], T.sem["arr%d_%d" % (t + 1, c)], T.sem.sent,
+            g.remote_dma(T.land[:, l + J:r + J], T.snd[:, l:r], T.sem["arr%d_%d" % (t + 1, c)], T.sem.sent,
                          pid, rid, topo.mask(core, dst))
             nsent[0] += len(topo.engines(core, dst))
-        op("G", f, [("ycs", i)], [])
+        op("G", f, [("snd", i)], [])
+
+    def over(i0, i1):
+        l, r = cols(i0)[0], cols(i1 - 1)[1]
+        gcopy(T.us[:, l:r], T.snd[:, l:r], r - l, [("snd", k) for k in range(i0, i1)], [("us", l // J)])
+
+    def shown(l, r):
+        op("V", lambda: V.tensor_tensor_scan(T.ycu[:, l:r], T.snd[:, l:r], T.us[:, l:r], 0.0, A.max, A.subtract),
+           [("us", t) for t in range(l // J, (r - 1) // J + 1)], [("ycu", l)])
+
+    def store_c(e, l, r, keys):
+        op(e, lambda: queue[e].dma_start(T.yc[0:112, l:r], T.ycs[16:128, l:r]), keys, [], "stored", 16)
+        op(e, lambda: queue[e].dma_start(T.yc[112:128, l:r], T.ycs[0:16, l:r]), keys, [], "stored", 16)
+
+    def ev_shown(l, r):
+        op("A", lambda: g.scalar.activation(T.ycs[:, l:r], T.ycu[:, l:r], Ident, bias=HALF, scale=1 / U), [("ycu", l)],
+           [("yc", l)])
+        if r < NY:
+            store_c("S", l, r, [("yc", l)])
 
     def ev_p(i):
-        t, c = divmod(i, NC)
+        c = i % NC
         a, b = span(i, 2)
-        if t < RO - 1:
-            op("V", lambda: V.tensor_tensor(T.plf[:, a:b], pp[c][:, 0:b - a], T.plf[:, a:b], A.add),
-               [], [("pp", c), ("plf", c)])
-        else:
-            op("V", lambda: V.tensor_scalar(T.tmp[:, 0:b - a], pp[c][:, 0:b - a], float(W), float(W), A.is_ge, A.mult),
-               [], [("pp", c), "tmp"])
+        out = T.plf[:, a:b] if i < NQ - NC else pp[c][:, 0:b - a]
+        op("V", lambda: V.tensor_tensor(out, pp[c][:, 0:b - a], T.plf[:, a:b], A.add), [], [("pp", c), ("plf", c)])
 
-    def ev_o(i):
-        t, c = divmod(i, NC)
+    def offsets(i):
         a, b = span(i, 2)
-        if t < RO - 1:
-            op("V", lambda: V.tensor_scalar(T.off[:, a:b], T.plf[:, a:b], -(RO - 1 - t) * CM, None, A.add),
-               [("plf", c)], [("off", c)])
-            return
-        op("V", lambda: V.tensor_tensor(T.yo[:, a:b], pp[c][:, 0:b - a], T.tmp[:, 0:b - a], A.subtract),
-           ["tmp"], [("pp", c), ("yo", c)])
+        gcopy(T.off[:, a:b], T.plf[:, a:b], b - a, [("plf", i % NC)], [("off", i % NC)])
+
+    def ev_w(i):
+        c = i % NC
+        a, b = span(i, 2)
+        op("V", lambda: V.tensor_scalar(T.tmp[:, a:b], pp[c][:, 0:b - a], float(W), float(W), A.is_ge, A.mult),
+           [], [("pp", c), ("tmp", c)])
+
+    def ev_y(i):
+        c = i % NC
+        a, b = span(i, 2)
+        op("V", lambda: V.tensor_tensor(T.yo[:, a:b], pp[c][:, 0:b - a], T.tmp[:, a:b], A.subtract),
+           [("tmp", c)], [("pp", c), ("yo", c)])
         if c >= NC - 2:
             c0 = 0 if c == NC - 2 else c
             op("S", lambda: g.sync.dma_start(T.yp[:, 2 * J0[c0]:b], T.yo[:, 2 * J0[c0]:b]),
                [("yo", k) for k in range(c0, c + 1)], [], "stored", 16)
 
-    def store_c(e, i0, i1):
-        cs = slice(cols(i0)[0], cols(i1 - 1)[1])
-        keys = [("ycs", k) for k in range(i0, i1)]
-        op(e, lambda: queue[e].dma_start(T.yc[0:112, cs], T.ycs[16:128, cs]), keys, [], "stored", 16)
-        op(e, lambda: queue[e].dma_start(T.yc[112:128, cs], T.ycs[0:16, cs]), keys, [], "stored", 16)
-
     gather("A", 0)
     gather("V", 0)
-    inject(0)
-    def out_c(i):
-        ev_c(i)
-        if i < NQ - NC:
-            send(i)
-        if i == NQ - 3:
-            store_c("S", 0, NQ - 2)
-        if i == NQ - 1:
-            store_c("A", NQ - 2, NQ)
-
-    for i in range(NQ):
-        more = i + 1 < NQ
-        if i >= NQ - NC:
-            mm_old(i)
+    op("V", lambda: V.tensor_scalar(T.land[:, 0:J], T.cin[:], LIFT - HALF, U, A.add, A.mult), ["cin"],
+       [("land", c) for c in every])
+    mm_x(0, range(1, 15))
+    fix(0)
+    mm_x(0, [0])
+    for i in range(NQ - 1):
+        t, c = divmod(i, NC)
+        gather("A", i + 1)
+        if i - 1 in SHOW:
+            ev_shown(*SHOW[i - 1])
         scan(i)
-        mm_v(i)
-        if i >= 1:
-            ev_p(i - 1)
-            if ORD == 1:
-                ev_o(i - 1)
-        floor16(i)
         mm_c(i)
         mm_q(i)
-        if i >= 1 and ORD == 0:
-            ev_o(i - 1)
-        if more:
-            gather("V", i + 1)
-            gather("A", i + 1)
-            inject(i + 1)
-        out_c(i)
-    ev_p(NQ - 1)
-    ev_o(NQ - 1)
+        if i >= 1:
+            ev_p(i - 1)
+        if 1 <= i <= NQ - NC:
+            offsets(i - 1)
+        cast(i)
+        gather("V", i + 1)
+        if i > NQ - NC:
+            ev_w(i - 1)
+        ev_d(i)
+        if i in SHOW:
+            shown(*SHOW[i])
+        if i + 2 == NQ:
+            mm_old(i + 1)
+        mm_s(i)
+        mm_x(i + 1, range(1, 15))
+        fix(i + 1)
+        mm_x(i + 1, [0])
+        ev_c(i)
+        if i > NQ - NC:
+            ev_y(i - 1)
+        if i < NQ - NC:
+            send(i)
+        if c == NC - 1 or i == NQ - 2:
+            over(t * NC, i + 1)
+    i = NQ - 1
+    scan(i)
+    mm_c(i)
+    mm_q(i)
+    cast(i)
+    ev_p(i - 1)
+    ev_d(i)
+    mm_s(i)
+    last_c(0)
+    ev_w(i - 1)
+    last_c(1)
+    shown(*SHOW[i])
+    ev_shown(*SHOW[i])
+    ev_y(i - 1)
+    last_c(2)
+    store_c("A", (RO - 1) * J, RO * J, [("yc", (RO - 1) * J), ("ycs", i)])
+    ev_w(i)
+    ev_y(i)
 
     g.wait_ge(T.sem.sent, nsent[0])
     for name in ("sG", "sA", "sP", "sV", "stored"):

from concourse.mybir import AluOpType, ActivationFunctionType

NR, W, S, J, RO = 8, 4096, 32, 128, 8
CH = (44, 42, 42)
ND = (9, 9, 9)
ND0 = (21, 7, 7)
NDL = (9, 7, 5)
NC = len(CH)
J0 = [sum(CH[:c]) for c in range(NC + 1)]
JM = max(CH)
EXT = 240 * (RO - 1)
U = 2.0 ** -28
UP = 2.0 ** 24
HALF = 7.5
LIFT = 64.0
NY = RO * J - CH[-1]
SHOW = {4 * NC: (0, 4 * J), (RO - 1) * NC: (4 * J, (RO - 1) * J), RO * NC - 1: ((RO - 1) * J, NY)}

SCRATCH = {
    "win": ("sbuf", [128, W + EXT], "bfloat16"),
    "pli": ("sbuf", [128, 256], "int32"),
    "plf": ("sbuf", [128, 256], "float32"),
    "off": ("sbuf", [128, 256], "uint16"),
    "xs": ("sbuf", [128, S * J], "bfloat16"),
    "vs": ("sbuf", [128, S * J + 16 * NC], "float16"),
    "msk": ("sbuf", [128, S * JM], "bfloat16"),
    "cin": ("sbuf", [128, J], "bfloat16"),
    "land": ("sbuf", [128, RO * J], "bfloat16"),
    "snd": ("sbuf", [128, NY], "bfloat16"),
    "us": ("sbuf", [128, NY], "float16"),
    "ycu": ("sbuf", [128, NY], "bfloat16"),
    "ycs": ("sbuf", [128, RO * J], "bfloat16"),
    "ds": ("sbuf", [128, 2 * JM], "float16"),
    "tmp": ("sbuf", [128, 256], "float32"),
    "tmc": ("sbuf", [128, CH[-1]], "float32"),
    "yo": ("sbuf", [128, 256], "float32"),
    "pcol": ("sbuf", [128, 1], "int32"),
    "gint": ("sbuf", [128, 1], "int32"),
    "rint": ("sbuf", [128, 1], "int32"),
    "g15": ("sbuf", [128, 1], "float32"),
    "gnum": ("sbuf", [128, 1], "float32"),
    "not0": ("sbuf", [128, 1], "float32"),
    "back": ("sbuf", [128, 1], "float32"),
    "idf": ("sbuf", [128, 128], "bfloat16"),
    "iw": ("sbuf", [128, 144], "bfloat16"),
    "wq": ("sbuf", [128, 144], "bfloat16"),
    "wl": ("sbuf", [128, 144], "bfloat16"),
    "idn": ("sbuf", [128, 128], "float32"),
}
for _n in ("ig", "sa", "shx", "shq", "shv", "one", "ones", "onex", "tri"):
    SCRATCH[_n] = ("sbuf", [128, 128], "bfloat16")
for _n in ["pc0", "pc1", "pd0", "pd1"] + ["pp%d" % _c for _c in range(NC)]:
    SCRATCH[_n] = ("psum", [128, 512], "float32")
SEMAPHORES = (["sV", "sP", "sA", "sG", "dring", "dext", "dplace", "dcarry", "stored", "sent"]
              + ["arr%d_%d" % (t, c) for t in range(1, RO) for c in range(NC)])


def rank_program(g, core, T, topo):
    rank = T.rank_of(core)
    if rank is None:
        return
    A = AluOpType
    Ident = ActivationFunctionType.Identity
    queue = {"V": g.vector, "P": g.tensor, "A": g.scalar, "G": g, "S": g.sync}
    known = {e: {} for e in queue}
    count = {}
    lastw, readers = {}, {}
    serial = [0]

    def wait(e, tok):
        _, name, val, clock, _e = tok
        if known[e].get(name, 0) >= val:
            return
        queue[e].wait_ge(T.sem[name], val)
        known[e][name] = val
        for k, v in clock.items():
            if known[e].get(k, 0) < v:
                known[e][k] = v

    def op(e, fn, reads, writes, sem=None, n=1):
        toks = [lastw[k] for k in list(reads) + list(writes) if k in lastw]
        toks += [t for k in writes for t in readers.get(k, [])]
        for tok in sorted(toks, key=lambda t: -t[0]):
            if e == "P" and tok[4] == "P":
                continue
            wait(e, tok)
        ins = fn()
        if ins is None:
            return
        name = sem or "s" + e
        ins.then_inc(T.sem[name], n)
        count[name] = count.get(name, 0) + n
        serial[0] += 1
        tok = (serial[0], name, count[name], dict(known[e]), e)
        for k in reads:
            readers.setdefault(k, []).append(tok)
        for k in writes:
            lastw[k] = tok
            readers[k] = []

    V, P = g.vector, g.tensor
    pp = [T["pp%d" % c] for c in range(NC)]
    NQ = RO * NC
    every = range(NC)

    def span(i, m):
        c = i % NC
        return m * J0[c], m * J0[c + 1]

    def vspan(i):
        a, b = span(i, S)
        return a + 16 * (i % NC + 1), b + 16 * (i % NC + 1)

    def cols(i):
        t, c = divmod(i, NC)
        return t * J + J0[c], t * J + J0[c + 1]

    op("A", lambda: g.scalar.dma_start(T.pli[:], T.place[:]), [], ["pli"], "dplace", 16)
    op("S", lambda: g.sync.dma_start(T.win[:, 0:W], T.ring[:]), [], ["win"], "dring", 16)
    op("A", lambda: g.scalar.dma_start(T.cin[:], T.carry[:]), [], ["cin"], "dcarry", 16)
    op("S", lambda: g.sync.dma_start(T.win[:, W:W + EXT], T.ring[:, 0:EXT]), [], ["ext"], "dext", 16)
    for i in range(NC, NQ):
        t, c = divmod(i, NC)
        src = T.cores[(rank - 1 - (t - 1) % (NR - 1)) % NR]
        serial[0] += 1
        lastw[("land", i)] = (serial[0], "arr%d_%d" % (t, c), len(topo.engines(src, core)), {}, "R")

    def iota(name, pattern, cm):
        op("G", lambda: g.iota(T[name][:], pattern, 0, cm, allow_small_or_imprecise_dtypes=True), [], [name])

    def scal(out, in0, s1, o1, s2=None, o2=None):
        col = [s1] if isinstance(s1, str) else []
        a1 = T[s1][:] if col else s1
        if o2 is None:
            op("V", lambda: V.tensor_scalar(T[out][:], T[in0][:], a1, None, o1), [in0] + col, [out])
        else:
            op("V", lambda: V.tensor_scalar(T[out][:], T[in0][:], a1, s2, o1, o2), [in0] + col, [out])

    def times(out, in0, k):
        op("A", lambda: g.scalar.activation(T[out][:], T[in0][:], Ident, scale=k), [in0], [out])

    def keep(out, in0, cmp, fill, base):
        op("G", lambda: g.affine_select(T[out][:], T[in0][:], [[1, 128]], cmp, fill, base, -1), [in0], [out])

    def gcopy(out, in_, n, reads, writes):
        op("G", lambda: g.affine_select(out, in_, [[0, n]], A.is_ge, 0.0, 0, 0), reads, writes)

    op("G", lambda: g.iota(T.pcol[:], [[0, 1]], 0, 1), [], ["pcol"])
    iota("iw", [[1, 144]], 0)
    iota("ig", [[16, 8], [0, 16]], 0)
    iota("idf", [[1, 128]], -1)
    op("V", lambda: V.memset(T.msk[:], 1.0), [], ["msk"])
    scal("gint", "pcol", 112, A.bitwise_and)
    scal("rint", "pcol", 15, A.bitwise_and)
    op("V", lambda: V.memset(T.msk[:, 0:S * JM:S], 0.0), [], ["msk"])
    scal("g15", "gint", 15.0, A.add)
    scal("gnum", "gint", 0.0, A.add)
    scal("not0", "rint", 0.0, A.is_gt)
    scal("wl", "iw", "g15", A.is_equal, 1 / U, A.mult)
    scal("one", "ig", "gnum", A.is_equal)
    scal("back", "rint", 0.0, A.is_equal, 16 * HALF, A.mult)
    scal("sa", "idf", 16.0, A.is_equal)
    scal("ones", "one", "not0", A.mult)
    op("V", lambda: V.memset(T.msk[:, S - 1:S * JM:S], UP), [], ["msk"])
    op("V", lambda: V.tensor_copy(T.off[:], T.pli[:]), ["pli"], [("off", c) for c in every])
    keep("shx", "sa", A.not_equal, 1.0, 112)
    keep("tri", "one", A.is_ge, 0.0, 0)
    times("wq", "wl", -1.0)
    times("onex", "one", 1 / U)
    times("shq", "shx", -1.0)
    times("shv", "shx", 1 / UP)
    gcopy(T.plf[:], T.pli[:], 2 * J, ["pli"], [("plf", c) for c in every])
    keep("idn", "one", A.is_equal, 0.0, 0)

    def nd(i):
        return ND0[i] if i < NC else NDL[i % NC] if i >= NQ - NC else ND[i % NC]

    def gather(e, i):
        t, c = divmod(i, NC)
        a, b = (J0[c], J0[c + 1] - nd(i)) if e == "A" else (J0[c + 1] - nd(i), J0[c + 1])
        out = T.xs[:, S * a:S * b]
        src = T.win[:, 0:W + 240 * t].indirect(T.off[:, 2 * a:2 * b])
        reads = ["win", ("off", c)] + (["ext"] if t else [])
        if e == "A":
            op("A", lambda: g.scalar.activation(out, src, Ident, scale=U), reads, [("xa", c)])
        else:
            op("V", lambda: V.tensor_scalar(out, src, U, None, A.mult), reads, [("xv", c)])

    def cast(i):
        l, r = cols(i)
        a, b = vspan(i)
        gcopy(T.vs[:, a - 1:b - 1:S], T.land[:, l:r], r - l, [("land", i)], [("vt", i % NC)])

    def xk(i):
        return [("xa", i % NC), ("xv", i % NC)]

    def fix(i):
        a, b = span(i, S)
        l, r = cols(i)
        op("V", lambda: V.tensor_tensor_scan(T.xs[:, a:b:S], T.xs[:, a:b:S], T.land[:, l:r], 1.0, A.min, A.add),
           [("land", i)] + xk(i), [("x0", i % NC)])

    def scan(i):
        a, b = span(i, S)
        l, r = vspan(i)
        op("V", lambda: V.tensor_tensor_scan(T.vs[:, l:r], T.msk[:, 0:b - a], T.xs[:, a:b], 0.0, A.mult, A.add),
           ["msk", ("x0", i % NC)] + xk(i), [("v", i % NC), ("vt", i % NC)])

    def mm_old(i):
        c = i % NC
        a, b = span(i, 2)
        op("P", lambda: P.matmul(pp[c][:, 0:b - a], T.idn[:], T.plf[:, a:b], True, False), ["idn", ("plf", c)], [("pp", c)])

    def mm_x(i, stages):
        c = i % NC
        a, b = span(i, S)
        pd = "pd%d" % (i % 2)

        def f():
            for r in stages:
                ins = P.matmul(T[pd][:, 0:2 * CH[c]], T.wl[:, 14 - r:142 - r], T.xs[:, a + r:b:16], r == 1, r == 0)
            return ins
        op("P", f, ["wl"] + xk(i) + ([("x0", c)] if 0 in stages else []), [pd])

    def ev_d(i):
        pd, n = "pd%d" % (i % 2), 2 * CH[i % NC]
        op("V", lambda: V.tensor_scalar(T.ds[:, 0:n], T[pd][:, 0:n], T.back[:], None, A.add), ["back"], [pd, "ds"])

    def mm_s(i):
        c = i % NC
        a, b = vspan(i)
        l, r = cols(i)
        n = 2 * CH[c]

        def f():
            P.matmul(pp[c][:, 0:n:2], T.wl[:, 15:143], T.land[:, l:r], False, False)
            P.matmul(pp[c][:, 1:n:2], T.onex[:], T.xs[:, S * J0[c] + 15:S * J0[c + 1]:S], False, False)
            P.matmul(pp[c][:, 0:n], T.wq[:, 15:143], T.vs[:, a - 1:b - 1:16], False, False)
            P.matmul(pp[c][:, 1:n:2], T.ones[:], T.ds[:, 0:n:2], False, False)
            return P.matmul(pp[c][:, 0:n], T.tri[:], T.ds[:, 0:n], False, True)
        op("P", f, ["wq", "wl", "onex", "ones", "tri", "ds", ("land", i), ("v", c), ("vt", c)] + xk(i), [("pp", c)])

    def mm_q(i):
        c = i % NC
        a, b = vspan(i)
        n = 2 * CH[c]

        def f():
            for r in range(1, 16):
                ins = P.matmul(pp[c][:, 0:n], T.wq[:, 15 - r:143 - r], T.vs[:, a + r - 1:b:16], r == 1 and i < NQ - 1, False)
            return ins
        op("P", f, ["wq", ("v", c)], [("pp", c)])

    def mm_c(i):
        c = i % NC
        a, b = span(i, S)
        l, r = vspan(i)
        pc = "pc%d" % (i % 2)

        def f():
            P.matmul(T[pc][:, 0:CH[c]], T.shx[:], T.xs[:, a + S - 1:b:S], True, False)
            P.matmul(T[pc][:, 0:CH[c]], T.shv[:], T.vs[:, l + S - 1:r:S], False, False)
            return P.matmul(T[pc][:, 0:CH[c]], T.shq[:], T.vs[:, l + S - 2:r:S], False, True)
        op("P", f, ["shx", "shv", "shq"] + xk(i) + [("v", c), ("vt", c)], [pc])

    def ev_c(i):
        l, r = cols(i)
        pc = "pc%d" % (i % 2)
        op("V", lambda: V.tensor_scalar(T.snd[:, l:r], T[pc][:, 0:r - l], LIFT * U, None, A.add), [], [pc, ("snd", i)])

    def last_c(k):
        n, pc = CH[-1], "pc%d" % ((NQ - 1) % 2)
        if k == 0:
            op("V", lambda: V.tensor_scalar(T.tmc[:], T[pc][:, 0:n], 8 * U, 16 * U, A.is_ge, A.mult), [], [pc, "tmc"])
        if k == 1:
            op("V", lambda: V.tensor_tensor(T.tmc[:], T[pc][:, 0:n], T.tmc[:], A.subtract), [], [pc, "tmc"])
        if k == 2:
            op("V", lambda: V.tensor_scalar(T.ycs[:, NY:RO * J], T.tmc[:], 1 / U, HALF, A.mult, A.add), ["tmc"],
               [("ycs", NQ - 1)])

    nsent = [0]

    def send(i):
        t, c = divmod(i, NC)
        dst = T.cores[(rank + 1 + t % (NR - 1)) % NR]
        rid, pid = topo.addr(dst, core)
        l, r = cols(i)

        def f():
            g.remote_dma(T.land[:, l + J:r + J], T.snd[:, l:r], T.sem["arr%d_%d" % (t + 1, c)], T.sem.sent,
                         pid, rid, topo.mask(core, dst))
            nsent[0] += len(topo.engines(core, dst))
        op("G", f, [("snd", i)], [])

    def over(i0, i1):
        l, r = cols(i0)[0], cols(i1 - 1)[1]
        gcopy(T.us[:, l:r], T.snd[:, l:r], r - l, [("snd", k) for k in range(i0, i1)], [("us", l // J)])

    def shown(l, r):
        op("V", lambda: V.tensor_tensor_scan(T.ycu[:, l:r], T.snd[:, l:r], T.us[:, l:r], 0.0, A.max, A.subtract),
           [("us", t) for t in range(l // J, (r - 1) // J + 1)], [("ycu", l)])

    def store_c(e, l, r, keys):
        op(e, lambda: queue[e].dma_start(T.yc[0:112, l:r], T.ycs[16:128, l:r]), keys, [], "stored", 16)
        op(e, lambda: queue[e].dma_start(T.yc[112:128, l:r], T.ycs[0:16, l:r]), keys, [], "stored", 16)

    def ev_shown(l, r):
        op("A", lambda: g.scalar.activation(T.ycs[:, l:r], T.ycu[:, l:r], Ident, bias=HALF, scale=1 / U), [("ycu", l)],
           [("yc", l)])
        if r < NY:
            store_c("S", l, r, [("yc", l)])

    def ev_p(i):
        c = i % NC
        a, b = span(i, 2)
        out = T.plf[:, a:b] if i < NQ - NC else pp[c][:, 0:b - a]
        op("V", lambda: V.tensor_tensor(out, pp[c][:, 0:b - a], T.plf[:, a:b], A.add), [], [("pp", c), ("plf", c)])

    def offsets(i):
        a, b = span(i, 2)
        gcopy(T.off[:, a:b], T.plf[:, a:b], b - a, [("plf", i % NC)], [("off", i % NC)])

    def ev_w(i):
        c = i % NC
        a, b = span(i, 2)
        op("V", lambda: V.tensor_scalar(T.tmp[:, a:b], pp[c][:, 0:b - a], float(W), float(W), A.is_ge, A.mult),
           [], [("pp", c), ("tmp", c)])

    def ev_y(i):
        c = i % NC
        a, b = span(i, 2)
        op("V", lambda: V.tensor_tensor(T.yo[:, a:b], pp[c][:, 0:b - a], T.tmp[:, a:b], A.subtract),
           [("tmp", c)], [("pp", c), ("yo", c)])
        if c >= NC - 2:
            c0 = 0 if c == NC - 2 else c
            op("S", lambda: g.sync.dma_start(T.yp[:, 2 * J0[c0]:b], T.yo[:, 2 * J0[c0]:b]),
               [("yo", k) for k in range(c0, c + 1)], [], "stored", 16)

    gather("A", 0)
    gather("V", 0)
    op("V", lambda: V.tensor_scalar(T.land[:, 0:J], T.cin[:], LIFT - HALF, U, A.add, A.mult), ["cin"],
       [("land", c) for c in every])
    mm_x(0, range(1, 15))
    fix(0)
    mm_x(0, [0])
    for i in range(NQ - 1):
        t, c = divmod(i, NC)
        gather("A", i + 1)
        if i - 1 in SHOW:
            ev_shown(*SHOW[i - 1])
        scan(i)
        mm_c(i)
        mm_q(i)
        if i >= 1:
            ev_p(i - 1)
        if 1 <= i <= NQ - NC:
            offsets(i - 1)
        cast(i)
        gather("V", i + 1)
        if i > NQ - NC:
            ev_w(i - 1)
        ev_d(i)
        if i in SHOW:
            shown(*SHOW[i])
        if i + 2 == NQ:
            mm_old(i + 1)
        mm_s(i)
        mm_x(i + 1, range(1, 15))
        fix(i + 1)
        mm_x(i + 1, [0])
        ev_c(i)
        if i > NQ - NC:
            ev_y(i - 1)
        if i < NQ - NC:
            send(i)
        if c == NC - 1 or i == NQ - 2:
            over(t * NC, i + 1)
    i = NQ - 1
    scan(i)
    mm_c(i)
    mm_q(i)
    cast(i)
    ev_p(i - 1)
    ev_d(i)
    mm_s(i)
    last_c(0)
    ev_w(i - 1)
    last_c(1)
    shown(*SHOW[i])
    ev_shown(*SHOW[i])
    ev_y(i - 1)
    last_c(2)
    store_c("A", (RO - 1) * J, RO * J, [("yc", (RO - 1) * J), ("ycs", i)])
    ev_w(i)
    ev_y(i)

    g.wait_ge(T.sem.sent, nsent[0])
    for name in ("sG", "sA", "sP", "sV", "stored"):
        g.wait_ge(T.sem[name], count[name])
